import numpy as np
import ml_dtypes


def mxq(x, axis, fmt="e4m3"):
    dtype, down = {"e4m3": (ml_dtypes.float8_e4m3fn, 7), "e5m2": (ml_dtypes.float8_e5m2, 14)}[fmt]
    v = np.moveaxis(np.asarray(x, np.float32).astype(ml_dtypes.bfloat16).astype(np.float64), axis, -1)
    blocks = v.reshape(v.shape[:-1] + (-1, 32))
    amax = np.abs(blocks).max(-1, keepdims=True)
    byte = np.maximum(np.where(amax > 0, np.frexp(amax)[1] - 1 + 127, 0) - down, 1)
    scale = np.exp2(byte - 127.0)
    codes = (blocks / scale).astype(np.float32).astype(dtype).astype(np.float64)
    return np.moveaxis((codes * scale).reshape(v.shape), -1, axis)


WIDE = False


def mx_kscale(k):
    if not WIDE:
        return np.ones(k)
    levels = np.array([10, -10, 5, -5, 0])
    if k % 512:
        return np.exp2(np.random.permutation(np.resize(levels, k // 32))).repeat(32)
    a = np.empty((k // 512, 16))
    for p in range(k // 512):
        a[p, :8] = np.random.permutation(np.resize(levels, 8))
        for g in range(8):
            far = levels[np.abs(levels - a[p, g]) >= 10]
            a[p, g + 8] = far[np.random.randint(len(far))]
    return np.exp2(a.ravel()).repeat(32)


def f64(x):
    return np.asarray(x).astype(np.float64)


def striped(idx):
    return np.tile(idx.reshape(-1, 16).T, (8, 1)).astype(np.uint16)


def unstriped(offs):
    return offs[:16].T.reshape(-1).astype(np.int64)


def pack_weight(w):
    k, n = w.shape
    w = f64(np.asarray(w, np.float32).astype(ml_dtypes.bfloat16)).reshape(k // 32, 32, n)
    amax = np.abs(w).max(1)
    byte = np.clip(np.where(amax > 0, np.frexp(amax)[1] - 1 + 127 - 7, 1), 1, 254)
    scaled = (w * np.exp2(127.0 - byte)[:, None, :]).reshape(k, n).astype(np.float32)
    words = np.ascontiguousarray(scaled.reshape(k // 512, 128, 4, n).transpose(0, 1, 3, 2)).astype(ml_dtypes.float8_e4m3fn).view(np.uint8)
    return words, np.ascontiguousarray(byte.astype(np.uint8).reshape(k // 512, 16, n))


def unpack_weight(words, scales):
    g, p, n, _ = words.shape
    vals = np.ascontiguousarray(words).view(ml_dtypes.float8_e4m3fn).astype(np.float64) * np.repeat(np.exp2(scales.astype(np.float64) - 127.0), 8, axis=1)[..., None]
    return vals.transpose(0, 1, 3, 2).reshape(g * 512, n)


E2M1 = np.array([0.0, 0.5, 1.0, 1.5, 2.0, 3.0, 4.0, 6.0, -0.0, -0.5, -1.0, -1.5, -2.0, -3.0, -4.0, -6.0])


def pack_fp4(w):
    k, n = w.shape
    w = f64(np.asarray(w, np.float32).astype(ml_dtypes.bfloat16)).reshape(k // 32, 32, n)
    amax = np.abs(w).max(1)
    mant, ex = np.frexp(amax / 6.0)
    byte = np.clip(np.where(amax > 0, np.where(mant > 0.5, ex, ex - 1) + 127, 1), 1, 254)
    scaled = (w * np.exp2(127.0 - byte)[:, None, :]).reshape(k, n).astype(np.float32)
    c = np.ascontiguousarray(scaled.reshape(k // 512, 128, 4, n).transpose(0, 1, 3, 2)).astype(ml_dtypes.float4_e2m1fn).view(np.uint8) & 0xF
    words = (c[..., 0::2] | (c[..., 1::2] << 4)).reshape(k // 512, 128, 2 * n)
    return np.ascontiguousarray(words), np.ascontiguousarray(byte.astype(np.uint8).reshape(k // 512, 16, n))


def unpack_fp4(words, scales):
    g, _, n = scales.shape
    words = np.ascontiguousarray(words).reshape(g, 128, n, 2)
    nib = np.empty((g, 128, n, 4), np.uint8)
    nib[..., 0::2] = words & 0xF
    nib[..., 1::2] = words >> 4
    vals = E2M1[nib] * np.repeat(np.exp2(scales.astype(np.float64) - 127.0), 8, axis=1)[..., None]
    return vals.transpose(0, 1, 3, 2).reshape(g * 512, n)


def planes(y):
    n, m = y.shape
    v = y.astype(np.float32).astype(ml_dtypes.bfloat16).astype(np.float64).reshape(n // 32, 32, m)
    top = np.abs(v).max(1)
    byte = np.clip(np.where(top > 0, np.frexp(top)[1] - 1 + 127 - 7, 1), 1, 254)
    codes = (v * np.exp2(127.0 - byte)[:, None, :]).reshape(n, m).astype(np.float32).astype(ml_dtypes.float8_e4m3fn).view(np.uint8)
    words = codes.reshape(n // 512, 128, 4, m).transpose(0, 1, 3, 2)
    return np.ascontiguousarray(words), np.ascontiguousarray(byte.astype(np.uint8).reshape(n // 512, 16, m))


K, T, S, N, H, U = 1024, 1024, 512, 512, 512, 1024


def setup_inputs():
    n = np.random.standard_normal
    s = mx_kscale(K)[:, None]
    u = mx_kscale(H)
    packed_xT = pack_weight(n((K, T)) * s)
    packed_w1 = pack_fp4(n((K, N)) / np.sqrt(K) / s)
    packed_w2 = pack_fp4(n((K, N)) / np.sqrt(K) / s)
    packed_w3 = pack_fp4(n((H, N)) / np.sqrt(H) / u[:, None])
    return {
        "x_words": packed_xT[0],
        "x_scales": packed_xT[1],
        "w1_words": packed_w1[0],
        "w1_scales": packed_w1[1],
        "w2_words": packed_w2[0],
        "w2_scales": packed_w2[1],
        "unit": (np.random.uniform(0.6, 1.4, (H, 1)) * u[:, None]).astype(np.float32),
        "w3_words": packed_w3[0],
        "w3_scales": packed_w3[1],
        "offs": striped(np.random.permutation(T)[:S]),
        "cl1": striped(np.random.permutation(np.concatenate([np.arange(S), np.random.randint(0, S, U - S)]))),
        "exc": striped(np.random.permutation(np.concatenate([np.arange(S), np.random.randint(0, S, U - S)]))),
        "def_": striped(np.random.permutation(np.concatenate([np.arange(S), np.random.randint(0, S, U - S)]))),
    }


def reference(x_words, x_scales, w1_words, w1_scales, w2_words, w2_scales, unit, w3_words, w3_scales, offs, cl1, exc, def_):
    xq = unpack_weight(x_words, x_scales)[:, unstriped(offs)]
    y = unpack_fp4(w1_words, w1_scales).T @ xq
    y_1 = y[:, unstriped(cl1)]
    z1 = unpack_fp4(w2_words, w2_scales).T @ xq
    zd = z1[:, unstriped(def_)]
    ze = z1[:, unstriped(exc)]
    hid = f64(unit) * np.minimum(y_1 * zd, ze)
    out_0 = unpack_fp4(w3_words, w3_scales).T @ mxq(hid, 0, "e4m3")
    return (out_0,) + planes(out_0)

@@ -1,0 +1,296 @@
+from contextlib import ExitStack
+
+import concourse.mybir as mybir
+
+K, T, S, N, H, U = 1024, 1024, 512, 512, 512, 1024
+FLOPS = 2 * (2 * K * N * S + H * N * U)
+
+F32 = mybir.dt.float32
+BF16 = mybir.dt.bfloat16
+I32 = mybir.dt.int32
+U32 = mybir.dt.uint32
+U16 = mybir.dt.uint16
+U8 = mybir.dt.uint8
+FP8X4 = mybir.dt.float8_e4m3fn_x4
+FP4X4 = mybir.dt.float4_e2m1fn_x4
+ALU = mybir.AluOpType
+ACT = mybir.ActivationFunctionType
+
+P = 128
+PACK = 4
+QUADS = 4
+PASSES = K // (P * PACK)
+HALF = S // 2
+BANK = 512
+CHUNKS = (256, 256, 256, 128, 128)
+RUN = 2
+
+
+def tile_picked_ywarrnt_min_po_kernel(
+    tc, x_words, x_scales, w1_words, w1_scales, w2_words, w2_scales, unit, w3_words, w3_scales,
+    offs, cl1, exc, def_, out_0, out_1, out_2,
+):
+    nc = tc.nc
+    with ExitStack() as ctx:
+        keep = ctx.enter_context(tc.tile_pool(name="keep", bufs=1))
+        ring = ctx.enter_context(tc.tile_pool(name="ring", bufs=3))
+        psum = ctx.enter_context(tc.psum_pool(name="psum", bufs=8))
+
+        def load_list(name, src):
+            lst = keep.tile(list(src.shape), U16, name=name)
+            nc.sync.dma_start(lst[:], src)
+            return lst
+
+        def load_words(name, src):
+            passes = src.shape[0]
+            raw = keep.tile([P, passes * 2 * N], U8, name=name, align_bytes=64)
+            nc.sync.dma_start(
+                raw[:].bitcast(I32).rearrange("p (g c) -> p g c", g=passes),
+                src.rearrange("g p c -> p g c").bitcast(I32),
+            )
+            return raw
+
+        def zeroed(name, width, engine):
+            plane = keep.tile([P, width], U8, name=name, align_bytes=64)
+            engine.memset(plane[:].bitcast(I32), 0)
+            return plane
+
+        def load_scales(raw, src):
+            passes = src.shape[0]
+            for q in range(QUADS):
+                nc.sync.dma_start(
+                    raw[32 * q : 32 * q + 4, :].bitcast(I32).rearrange("p (g c) -> p g c", g=passes),
+                    src[:, 4 * q : 4 * q + 4, :].rearrange("g r c -> r g c").bitcast(I32),
+                )
+
+        def deal_words(name, raw, engine):
+            dealt = keep.tile(list(raw.shape), U8, name=name, align_bytes=64)
+            engine.tensor_copy(
+                dealt[:].rearrange("p (t m b) -> p m t b", t=PACK, b=2),
+                raw[:].rearrange("p (m t b) -> p m t b", t=PACK, b=2),
+            )
+            return dealt
+
+        def deal_scales(name, raw, engine):
+            dealt = keep.tile(list(raw.shape), U8, name=name, align_bytes=64)
+            engine.tensor_copy(
+                dealt[:].rearrange("p (t m) -> p m t", t=PACK),
+                raw[:].rearrange("p (m t) -> p m t", t=PACK),
+            )
+            return dealt
+
+        def stationary(words, scales, passes, t, g):
+            at = (t * passes + g) * P
+            return words[:, 2 * at : 2 * (at + P)].bitcast(FP4X4), scales[:, at : at + P]
+
+        x_scale_rows = zeroed("x_scale_rows", T, nc.vector)
+        w2_scale_rows = zeroed("w2_scale_rows", PASSES * N, nc.vector)
+        w1_scale_rows = zeroed("w1_scale_rows", PASSES * N, nc.gpsimd)
+        xq_scales_1 = zeroed("xq_scales_1", S, nc.gpsimd)
+        w3_scale_rows = zeroed("w3_scale_rows", N, nc.gpsimd)
+
+        w2_raw = load_words("w2_raw", w2_words)
+        offs_sb = load_list("offs_sb", offs)
+        for q in range(QUADS):
+            nc.sync.dma_start(
+                x_scale_rows[32 * q : 32 * q + 4 * PASSES, :].bitcast(I32),
+                x_scales[:, 4 * q : 4 * q + 4, :].bitcast(I32),
+            )
+        x_table = []
+        for g in range(PASSES):
+            table = keep.tile([P, T], I32, name=f"x_table{g}", align_bytes=64)
+            nc.sync.dma_start(table[:], x_words[g].rearrange("p c r -> p (c r)").bitcast(I32))
+            x_table.append(table)
+        load_scales(w2_scale_rows, w2_scales)
+        unit_sb = keep.tile([P, PACK], F32, name="unit_sb")
+        nc.sync.dma_start(unit_sb[:], unit.rearrange("(p t) o -> p (t o)", t=PACK))
+        w1_raw = load_words("w1_raw", w1_words)
+
+        unit_abs = keep.tile([P, PACK], F32, name="unit_abs")
+        nc.scalar.activation(unit_abs[:], unit_sb[:], ACT.Abs)
+        unit_sign = keep.tile([P, PACK], BF16, name="unit_sign")
+        nc.scalar.activation(unit_sign[:], unit_sb[:], ACT.Sign)
+
+        w2_dealt = deal_words("w2_dealt", w2_raw, nc.vector)
+        xq_scales_0 = keep.tile([P, S], U8, name="xq_scales_0", align_bytes=64)
+        nc.vector.tensor_copy(xq_scales_0[:], x_scale_rows[:].indirect(offs_sb[:]))
+        for q in range(QUADS):
+            nc.sync.dma_start(
+                xq_scales_1[32 * q : 32 * q + 4, :].bitcast(I32),
+                xq_scales_0[32 * q + 4 : 32 * q + 8, :].bitcast(I32),
+            )
+        xq_scales = (xq_scales_0, xq_scales_1)
+        def_sb = load_list("def_sb", def_)
+        load_scales(w1_scale_rows, w1_scales)
+        cl1_sb = load_list("cl1_sb", cl1)
+        exc_sb = load_list("exc_sb", exc)
+        w3_raw = load_words("w3_raw", w3_words)
+        load_scales(w3_scale_rows, w3_scales)
+
+        w2_scale_dealt = deal_scales("w2_scale_dealt", w2_scale_rows, nc.vector)
+
+        xq_words = {}
+
+        def first_product(acc, words, scales, t, h):
+            for g in range(PASSES):
+                lhsT, lhsT_scale = stationary(words, scales, PASSES, t, g)
+                nc.tensor.matmul_mx(
+                    acc, lhsT=lhsT, lhsT_scale=lhsT_scale,
+                    rhs=xq_words[g, h][:].bitcast(FP8X4),
+                    rhs_scale=xq_scales[g][:, h * HALF : (h + 1) * HALF],
+                    start=(g == 0), stop=(g == PASSES - 1),
+                )
+
+        z = [keep.tile([P, S], F32, name=f"z{t}") for t in range(PACK)]
+        y = [keep.tile([P, S], F32, name=f"y{t}") for t in range(PACK)]
+        for h in range(2):
+            for g in range(PASSES):
+                picked = keep.tile([P, HALF], U32, name=f"xq_words{g}{h}", align_bytes=64)
+                nc.vector.tensor_copy(
+                    picked[:],
+                    x_table[g][:].bitcast(U32).indirect(offs_sb[:, h * HALF // 16 : (h + 1) * HALF // 16]),
+                )
+                xq_words[g, h] = picked
+            for t0 in range(0, PACK, 2):
+                bank = psum.tile([P, BANK], F32, name="bank")
+                for t in (t0, t0 + 1):
+                    first_product(bank[:, (t - t0) * HALF : (t - t0 + 1) * HALF], w2_dealt, w2_scale_dealt, t, h)
+                for t in (t0, t0 + 1):
+                    nc.scalar.activation(
+                        z[t][:, h * HALF : (h + 1) * HALF],
+                        bank[:, (t - t0) * HALF : (t - t0 + 1) * HALF],
+                        ACT.Copy, scale=unit_abs[:, t : t + 1],
+                    )
+
+        w1_dealt = deal_words("w1_dealt", w1_raw, nc.vector)
+        w1_scale_dealt = deal_scales("w1_scale_dealt", w1_scale_rows, nc.vector)
+        for t in range(PACK):
+            bank = psum.tile([P, BANK], F32, name="bank")
+            for h in range(2):
+                first_product(bank[:, h * HALF : (h + 1) * HALF], w1_dealt, w1_scale_dealt, t, h)
+            nc.vector.tensor_copy(y[t][:], bank[:])
+        w3_dealt = deal_words("w3_dealt", w3_raw, nc.vector)
+        w3_scale_dealt = deal_scales("w3_scale_dealt", w3_scale_rows, nc.vector)
+
+        out_codes = keep.tile([P, U], U32, name="out_codes", align_bytes=64)
+        out_scales = keep.tile([P, U], U8, name="out_scales", align_bytes=64)
+        out_rows = out_0.rearrange("(p t) r -> p t r", t=PACK)
+        out_words = out_1[0].rearrange("p c r -> p (c r)").bitcast(I32)
+
+        starts = [sum(CHUNKS[:c]) for c in range(len(CHUNKS))]
+        st = [dict() for c in CHUNKS]
+
+        def entries(lst, c):
+            return lst[:, starts[c] // 16 : (starts[c] + CHUNKS[c]) // 16]
+
+        def planes(ap):
+            return ap.rearrange("p t (c i) -> p c t i", i=RUN)
+
+        def woven(ap):
+            return ap.rearrange("p (c i t) -> p c t i", i=RUN, t=PACK)
+
+        def gather_def(c):
+            st[c]["zd"] = []
+            for t in range(PACK):
+                zd = ring.tile([P, CHUNKS[c]], F32, name=f"zd{t}", bufs=1)
+                nc.scalar.activation(zd[:], z[t][:].indirect(entries(def_sb, c)), ACT.Copy)
+                st[c]["zd"].append(zd)
+            st[c]["prod"] = ring.tile([P, PACK, CHUNKS[c]], F32, name="prod")
+
+        def gather_exc(c):
+            ze = ring.tile([P, PACK, CHUNKS[c]], F32, name="ze", bufs=1)
+            for t in range(PACK):
+                nc.scalar.activation(ze[:, t, :], z[t][:].indirect(entries(exc_sb, c)), ACT.Copy)
+            st[c]["ze"] = ze
+
+        def gather_mult(c, t):
+            nc.vector.tensor_tensor(
+                st[c]["prod"][:, t, :], y[t][:].indirect(entries(cl1_sb, c)), st[c]["zd"][t][:], ALU.mult
+            )
+
+        def cut(c):
+            mag = ring.tile([P, PACK * CHUNKS[c]], BF16, name="mag", align_bytes=64)
+            nc.vector.tensor_tensor(woven(mag[:]), planes(st[c]["prod"][:]), planes(st[c]["ze"][:]), ALU.min)
+            st[c]["mag"] = mag
+
+        def signed(c):
+            n = CHUNKS[c]
+            hid = ring.tile([P, PACK * n], BF16, name="hid", align_bytes=64)
+            nc.vector.tensor_tensor(
+                hid[:].rearrange("p (r t) -> p r t", t=PACK),
+                st[c]["mag"][:].rearrange("p (r t) -> p r t", t=PACK),
+                unit_sign[:].unsqueeze(1).to_broadcast([P, n, PACK]),
+                ALU.mult,
+            )
+            st[c]["hid"] = hid
+
+        def last_product(c):
+            n = CHUNKS[c]
+            codes = ring.tile([P, n], U32, name="hid_codes", align_bytes=64)
+            scales = ring.tile([P, n], U8, name="hid_scales", align_bytes=64)
+            nc.vector.quantize_mx(codes[:].bitcast(FP8X4), scales[:], st[c]["hid"][:])
+            per_bank = BANK // n
+            banks = []
+            for t0 in range(0, PACK, per_bank):
+                bank = psum.tile([P, BANK], F32, name="bank")
+                for t in range(t0, t0 + per_bank):
+                    lhsT, lhsT_scale = stationary(w3_dealt, w3_scale_dealt, 1, t, 0)
+                    nc.tensor.matmul_mx(
+                        bank[:, (t - t0) * n : (t - t0 + 1) * n], lhsT=lhsT, lhsT_scale=lhsT_scale,
+                        rhs=codes[:].bitcast(FP8X4), rhs_scale=scales[:], start=True, stop=True,
+                    )
+                banks.append(bank)
+            st[c]["banks"] = banks
+
+        def leave_psum(c):
+            n = CHUNKS[c]
+            res = ring.tile([P, PACK * n], F32, name="res")
+            for b, bank in enumerate(st[c]["banks"]):
+                nc.scalar.copy(res[:, b * BANK : (b + 1) * BANK], bank[:])
+            res3 = res[:].rearrange("p (t r) -> p t r", t=PACK)
+            nc.sync.dma_start(out_rows[:, :, starts[c] : starts[c] + n], res3)
+            st[c]["res"] = res3
+
+        def rounded(c):
+            rnd = ring.tile([P, PACK * CHUNKS[c]], BF16, name="rnd", align_bytes=64)
+            nc.vector.tensor_copy(woven(rnd[:]), planes(st[c]["res"]))
+            st[c]["rnd"] = rnd
+
+        def hand_on(c):
+            cols = slice(starts[c], starts[c] + CHUNKS[c])
+            nc.vector.quantize_mx(out_codes[:, cols].bitcast(FP8X4), out_scales[:, cols], st[c]["rnd"][:])
+            nc.sync.dma_start(out_words[:, cols], out_codes[:, cols].bitcast(I32))
+
+        last = len(CHUNKS) - 1
+        for c in range(last + 3):
+            here, one_back, two_back = c <= last, 1 <= c <= last + 1, c >= 2
+            if here:
+                gather_def(c)
+            if two_back:
+                rounded(c - 2)
+            if here:
+                gather_mult(c, 0)
+            if one_back:
+                cut(c - 1)
+            if two_back:
+                hand_on(c - 2)
+            if here:
+                gather_mult(c, 1)
+            if one_back:
+                signed(c - 1)
+            if here:
+                gather_mult(c, 2)
+            if one_back:
+                last_product(c - 1)
+            if here:
+                gather_mult(c, 3)
+                gather_exc(c)
+            if one_back:
+                leave_psum(c - 1)
+
+        for q in range(QUADS):
+            queue = nc.sync if q % 2 == 0 else nc.scalar
+            queue.dma_start(
+                out_2[0, 4 * q : 4 * q + 4, :].bitcast(I32),
+                out_scales[32 * q : 32 * q + 4, :].bitcast(I32),
+            )

@@ -20,9 +20,10 @@ P = 128
 PACK = 4
 QUADS = 4
 PASSES = K // (P * PACK)
-HALF = S // 2
 BANK = 512
-CHUNKS = (256, 256, 256, 128, 128)
+CHUNKS = (384, 256, 256, 128)
+BLOCK = BANK // PACK
+ON_VECTOR = (2, 0, 0, 0)
 RUN = 2
 
 
@@ -50,8 +51,8 @@ def tile_picked_ywarrnt_min_po_kernel(
             )
             return raw
 
-        def zeroed(name, width, engine):
-            plane = keep.tile([P, width], U8, name=name, align_bytes=64)
+        def zeroed(name, width, engine, tag=""):
+            plane = keep.tile([P, width], U8, name=name, tag=tag, align_bytes=64)
             engine.memset(plane[:].bitcast(I32), 0)
             return plane
 
@@ -66,16 +67,16 @@ def tile_picked_ywarrnt_min_po_kernel(
         def deal_words(name, raw, engine):
             dealt = keep.tile(list(raw.shape), U8, name=name, align_bytes=64)
             engine.tensor_copy(
-                dealt[:].rearrange("p (t m b) -> p m t b", t=PACK, b=2),
-                raw[:].rearrange("p (m t b) -> p m t b", t=PACK, b=2),
+                dealt[:].bitcast(U16).rearrange("p (t m) -> p t m", t=PACK),
+                raw[:].bitcast(U16).rearrange("p (m t) -> p t m", t=PACK),
             )
             return dealt
 
         def deal_scales(name, raw, engine):
             dealt = keep.tile(list(raw.shape), U8, name=name, align_bytes=64)
             engine.tensor_copy(
-                dealt[:].rearrange("p (t m) -> p m t", t=PACK),
-                raw[:].rearrange("p (m t) -> p m t", t=PACK),
+                dealt[:].rearrange("p (t m) -> p t m", t=PACK),
+                raw[:].rearrange("p (m t) -> p t m", t=PACK),
             )
             return dealt
 
@@ -83,35 +84,26 @@ def tile_picked_ywarrnt_min_po_kernel(
             at = (t * passes + g) * P
             return words[:, 2 * at : 2 * (at + P)].bitcast(FP4X4), scales[:, at : at + P]
 
-        x_scale_rows = zeroed("x_scale_rows", T, nc.vector)
-        w2_scale_rows = zeroed("w2_scale_rows", PASSES * N, nc.vector)
-        w1_scale_rows = zeroed("w1_scale_rows", PASSES * N, nc.gpsimd)
+        x_scale_rows = zeroed("x_scale_rows", T, nc.gpsimd)
+        w2_scale_rows = zeroed("w2_scale_rows", PASSES * N, nc.vector, tag="shared")
         xq_scales_1 = zeroed("xq_scales_1", S, nc.gpsimd)
+        w1_scale_rows = zeroed("w1_scale_rows", PASSES * N, nc.vector)
         w3_scale_rows = zeroed("w3_scale_rows", N, nc.gpsimd)
 
-        w2_raw = load_words("w2_raw", w2_words)
         offs_sb = load_list("offs_sb", offs)
         for q in range(QUADS):
             nc.sync.dma_start(
                 x_scale_rows[32 * q : 32 * q + 4 * PASSES, :].bitcast(I32),
                 x_scales[:, 4 * q : 4 * q + 4, :].bitcast(I32),
             )
+        w2_raw = load_words("w2_raw", w2_words)
         x_table = []
         for g in range(PASSES):
             table = keep.tile([P, T], I32, name=f"x_table{g}", align_bytes=64)
             nc.sync.dma_start(table[:], x_words[g].rearrange("p c r -> p (c r)").bitcast(I32))
             x_table.append(table)
         load_scales(w2_scale_rows, w2_scales)
-        unit_sb = keep.tile([P, PACK], F32, name="unit_sb")
-        nc.sync.dma_start(unit_sb[:], unit.rearrange("(p t) o -> p (t o)", t=PACK))
-        w1_raw = load_words("w1_raw", w1_words)
 
-        unit_abs = keep.tile([P, PACK], F32, name="unit_abs")
-        nc.scalar.activation(unit_abs[:], unit_sb[:], ACT.Abs)
-        unit_sign = keep.tile([P, PACK], BF16, name="unit_sign")
-        nc.scalar.activation(unit_sign[:], unit_sb[:], ACT.Sign)
-
-        w2_dealt = deal_words("w2_dealt", w2_raw, nc.vector)
         xq_scales_0 = keep.tile([P, S], U8, name="xq_scales_0", align_bytes=64)
         nc.vector.tensor_copy(xq_scales_0[:], x_scale_rows[:].indirect(offs_sb[:]))
         for q in range(QUADS):
@@ -120,57 +112,53 @@ def tile_picked_ywarrnt_min_po_kernel(
                 xq_scales_0[32 * q + 4 : 32 * q + 8, :].bitcast(I32),
             )
         xq_scales = (xq_scales_0, xq_scales_1)
-        def_sb = load_list("def_sb", def_)
+
+        unit_sb = keep.tile([P, PACK], F32, name="unit_sb")
+        nc.sync.dma_start(unit_sb[:], unit.rearrange("(p t) o -> p (t o)", t=PACK))
+        w1_raw = load_words("w1_raw", w1_words)
         load_scales(w1_scale_rows, w1_scales)
+        def_sb = load_list("def_sb", def_)
         cl1_sb = load_list("cl1_sb", cl1)
         exc_sb = load_list("exc_sb", exc)
         w3_raw = load_words("w3_raw", w3_words)
         load_scales(w3_scale_rows, w3_scales)
 
-        w2_scale_dealt = deal_scales("w2_scale_dealt", w2_scale_rows, nc.vector)
+        unit_abs = keep.tile([P, PACK], F32, name="unit_abs")
+        nc.scalar.activation(unit_abs[:], unit_sb[:], ACT.Abs)
+        unit_sign = keep.tile([P, PACK], BF16, name="unit_sign")
+        nc.scalar.activation(unit_sign[:], unit_sb[:], ACT.Sign)
 
-        xq_words = {}
+        def picked_words(g, tag=""):
+            picked = keep.tile([P, S], U32, name=f"xq_words{g}", tag=tag, align_bytes=64)
+            nc.vector.tensor_copy(picked[:], x_table[g][:].bitcast(U32).indirect(offs_sb[:]))
+            return picked
 
-        def first_product(acc, words, scales, t, h):
+        def first_product(words, scales, t):
+            bank = psum.tile([P, BANK], F32, name="bank")
             for g in range(PASSES):
                 lhsT, lhsT_scale = stationary(words, scales, PASSES, t, g)
                 nc.tensor.matmul_mx(
-                    acc, lhsT=lhsT, lhsT_scale=lhsT_scale,
-                    rhs=xq_words[g, h][:].bitcast(FP8X4),
-                    rhs_scale=xq_scales[g][:, h * HALF : (h + 1) * HALF],
+                    bank[:], lhsT=lhsT, lhsT_scale=lhsT_scale,
+                    rhs=xq_words[g][:].bitcast(FP8X4), rhs_scale=xq_scales[g][:],
                     start=(g == 0), stop=(g == PASSES - 1),
                 )
+            return bank
+
+        w2_dealt = deal_words("w2_dealt", w2_raw, nc.vector)
+        xq_words = [picked_words(0)]
+        w2_scale_dealt = deal_scales("w2_scale_dealt", w2_scale_rows, nc.vector)
+        xq_words.append(picked_words(1, tag="shared"))
+        w1_dealt = deal_words("w1_dealt", w1_raw, nc.vector)
+        w1_scale_dealt = deal_scales("w1_scale_dealt", w1_scale_rows, nc.vector)
+        w3_dealt = deal_words("w3_dealt", w3_raw, nc.vector)
+        w3_scale_dealt = deal_scales("w3_scale_dealt", w3_scale_rows, nc.vector)
 
         z = [keep.tile([P, S], F32, name=f"z{t}") for t in range(PACK)]
         y = [keep.tile([P, S], F32, name=f"y{t}") for t in range(PACK)]
-        for h in range(2):
-            for g in range(PASSES):
-                picked = keep.tile([P, HALF], U32, name=f"xq_words{g}{h}", align_bytes=64)
-                nc.vector.tensor_copy(
-                    picked[:],
-                    x_table[g][:].bitcast(U32).indirect(offs_sb[:, h * HALF // 16 : (h + 1) * HALF // 16]),
-                )
-                xq_words[g, h] = picked
-            for t0 in range(0, PACK, 2):
-                bank = psum.tile([P, BANK], F32, name="bank")
-                for t in (t0, t0 + 1):
-                    first_product(bank[:, (t - t0) * HALF : (t - t0 + 1) * HALF], w2_dealt, w2_scale_dealt, t, h)
-                for t in (t0, t0 + 1):
-                    nc.scalar.activation(
-                        z[t][:, h * HALF : (h + 1) * HALF],
-                        bank[:, (t - t0) * HALF : (t - t0 + 1) * HALF],
-                        ACT.Copy, scale=unit_abs[:, t : t + 1],
-                    )
-
-        w1_dealt = deal_words("w1_dealt", w1_raw, nc.vector)
-        w1_scale_dealt = deal_scales("w1_scale_dealt", w1_scale_rows, nc.vector)
+        z_banks, y_banks = [], []
         for t in range(PACK):
-            bank = psum.tile([P, BANK], F32, name="bank")
-            for h in range(2):
-                first_product(bank[:, h * HALF : (h + 1) * HALF], w1_dealt, w1_scale_dealt, t, h)
-            nc.vector.tensor_copy(y[t][:], bank[:])
-        w3_dealt = deal_words("w3_dealt", w3_raw, nc.vector)
-        w3_scale_dealt = deal_scales("w3_scale_dealt", w3_scale_rows, nc.vector)
+            z_banks.append(first_product(w2_dealt, w2_scale_dealt, t))
+            y_banks.append(first_product(w1_dealt, w1_scale_dealt, t))
 
         out_codes = keep.tile([P, U], U32, name="out_codes", align_bytes=64)
         out_scales = keep.tile([P, U], U8, name="out_scales", align_bytes=64)
@@ -192,18 +180,25 @@ def tile_picked_ywarrnt_min_po_kernel(
         def gather_def(c):
             st[c]["zd"] = []
             for t in range(PACK):
-                zd = ring.tile([P, CHUNKS[c]], F32, name=f"zd{t}", bufs=1)
+                if c == 0:
+                    nc.scalar.activation(z[t][:], z_banks[t][:], ACT.Copy, scale=unit_abs[:, t : t + 1])
+                zd = ring.tile([P, CHUNKS[c]], F32, name=f"zd{t}", bufs=2)
                 nc.scalar.activation(zd[:], z[t][:].indirect(entries(def_sb, c)), ACT.Copy)
                 st[c]["zd"].append(zd)
             st[c]["prod"] = ring.tile([P, PACK, CHUNKS[c]], F32, name="prod")
 
         def gather_exc(c):
-            ze = ring.tile([P, PACK, CHUNKS[c]], F32, name="ze", bufs=1)
+            ze = ring.tile([P, PACK, CHUNKS[c]], F32, name="ze", bufs=2)
             for t in range(PACK):
-                nc.scalar.activation(ze[:, t, :], z[t][:].indirect(entries(exc_sb, c)), ACT.Copy)
+                if t < ON_VECTOR[c]:
+                    nc.vector.tensor_copy(ze[:, t, :], z[t][:].indirect(entries(exc_sb, c)))
+                else:
+                    nc.scalar.activation(ze[:, t, :], z[t][:].indirect(entries(exc_sb, c)), ACT.Copy)
             st[c]["ze"] = ze
 
         def gather_mult(c, t):
+            if c == 0:
+                nc.vector.tensor_copy(y[t][:], y_banks[t][:])
             nc.vector.tensor_tensor(
                 st[c]["prod"][:, t, :], y[t][:].indirect(entries(cl1_sb, c)), st[c]["zd"][t][:], ALU.mult
             )
@@ -229,27 +224,26 @@ def tile_picked_ywarrnt_min_po_kernel(
             codes = ring.tile([P, n], U32, name="hid_codes", align_bytes=64)
             scales = ring.tile([P, n], U8, name="hid_scales", align_bytes=64)
             nc.vector.quantize_mx(codes[:].bitcast(FP8X4), scales[:], st[c]["hid"][:])
-            per_bank = BANK // n
             banks = []
-            for t0 in range(0, PACK, per_bank):
-                bank = psum.tile([P, BANK], F32, name="bank")
-                for t in range(t0, t0 + per_bank):
+            for b0 in range(0, n, BLOCK):
+                bank = psum.tile([P, PACK, BLOCK], F32, name="bank")
+                for t in range(PACK):
                     lhsT, lhsT_scale = stationary(w3_dealt, w3_scale_dealt, 1, t, 0)
                     nc.tensor.matmul_mx(
-                        bank[:, (t - t0) * n : (t - t0 + 1) * n], lhsT=lhsT, lhsT_scale=lhsT_scale,
-                        rhs=codes[:].bitcast(FP8X4), rhs_scale=scales[:], start=True, stop=True,
+                        bank[:, t, :], lhsT=lhsT, lhsT_scale=lhsT_scale,
+                        rhs=codes[:, b0 : b0 + BLOCK].bitcast(FP8X4), rhs_scale=scales[:, b0 : b0 + BLOCK],
+                        start=True, stop=True,
                     )
                 banks.append(bank)
             st[c]["banks"] = banks
 
         def leave_psum(c):
             n = CHUNKS[c]
-            res = ring.tile([P, PACK * n], F32, name="res")
+            res = ring.tile([P, PACK, n], F32, name="res", bufs=len(CHUNKS))
             for b, bank in enumerate(st[c]["banks"]):
-                nc.scalar.copy(res[:, b * BANK : (b + 1) * BANK], bank[:])
-            res3 = res[:].rearrange("p (t r) -> p t r", t=PACK)
-            nc.sync.dma_start(out_rows[:, :, starts[c] : starts[c] + n], res3)
-            st[c]["res"] = res3
+                nc.scalar.copy(res[:, :, b * BLOCK : (b + 1) * BLOCK], bank[:])
+            nc.sync.dma_start(out_rows[:, :, starts[c] : starts[c] + n], res[:])
+            st[c]["res"] = res[:]
 
         def rounded(c):
             rnd = ring.tile([P, PACK * CHUNKS[c]], BF16, name="rnd", align_bytes=64)
@@ -262,18 +256,13 @@ def tile_picked_ywarrnt_min_po_kernel(
             nc.sync.dma_start(out_words[:, cols], out_codes[:, cols].bitcast(I32))
 
         last = len(CHUNKS) - 1
-        for c in range(last + 3):
-            here, one_back, two_back = c <= last, 1 <= c <= last + 1, c >= 2
+        for c in range(last + 4):
+            here, one_back, three_back = c <= last, 1 <= c <= last + 1, c >= 3
             if here:
                 gather_def(c)
-            if two_back:
-                rounded(c - 2)
-            if here:
                 gather_mult(c, 0)
             if one_back:
                 cut(c - 1)
-            if two_back:
-                hand_on(c - 2)
             if here:
                 gather_mult(c, 1)
             if one_back:
@@ -282,11 +271,15 @@ def tile_picked_ywarrnt_min_po_kernel(
                 gather_mult(c, 2)
             if one_back:
                 last_product(c - 1)
+                leave_psum(c - 1)
             if here:
                 gather_mult(c, 3)
+            if three_back:
+                rounded(c - 3)
+            if here:
                 gather_exc(c)
-            if one_back:
-                leave_psum(c - 1)
+            if three_back:
+                hand_on(c - 3)
 
         for q in range(QUADS):
             queue = nc.sync if q % 2 == 0 else nc.scalar

@@ -24,7 +24,7 @@ BANK = 512
 CHUNKS = (384, 256, 256, 128)
 BLOCK = BANK // PACK
 ON_VECTOR = (2, 0, 0, 0)
-RUN = 2
+RUN = 4
 
 
 def tile_picked_ywarrnt_min_po_kernel(
@@ -125,8 +125,12 @@ def tile_picked_ywarrnt_min_po_kernel(
 
         unit_abs = keep.tile([P, PACK], F32, name="unit_abs")
         nc.scalar.activation(unit_abs[:], unit_sb[:], ACT.Abs)
-        unit_sign = keep.tile([P, PACK], BF16, name="unit_sign")
-        nc.scalar.activation(unit_sign[:], unit_sb[:], ACT.Sign)
+        unit_sign = keep.tile([P, BLOCK * PACK], BF16, name="unit_sign")
+        nc.scalar.activation(
+            unit_sign[:].rearrange("p (r t) -> p r t", t=PACK),
+            unit_sb[:].unsqueeze(1).to_broadcast([P, BLOCK, PACK]),
+            ACT.Sign,
+        )
 
         def picked_words(g, tag=""):
             picked = keep.tile([P, S], U32, name=f"xq_words{g}", tag=tag, align_bytes=64)
@@ -212,9 +216,9 @@ def tile_picked_ywarrnt_min_po_kernel(
             n = CHUNKS[c]
             hid = ring.tile([P, PACK * n], BF16, name="hid", align_bytes=64)
             nc.vector.tensor_tensor(
-                hid[:].rearrange("p (r t) -> p r t", t=PACK),
-                st[c]["mag"][:].rearrange("p (r t) -> p r t", t=PACK),
-                unit_sign[:].unsqueeze(1).to_broadcast([P, n, PACK]),
+                hid[:].rearrange("p (b e) -> p b e", e=BLOCK * PACK),
+                st[c]["mag"][:].rearrange("p (b e) -> p b e", e=BLOCK * PACK),
+                unit_sign[:].unsqueeze(1).to_broadcast([P, n // BLOCK, BLOCK * PACK]),
                 ALU.mult,
             )
             st[c]["hid"] = hid

@@ -51,6 +51,11 @@ def tile_picked_ywarrnt_min_po_kernel(
             )
             return raw
 
+        def load_table(g):
+            table = keep.tile([P, T], I32, name=f"x_table{g}", align_bytes=64)
+            nc.sync.dma_start(table[:], x_words[g].rearrange("p c r -> p (c r)").bitcast(I32))
+            return table
+
         def zeroed(name, width, engine, tag=""):
             plane = keep.tile([P, width], U8, name=name, tag=tag, align_bytes=64)
             engine.memset(plane[:].bitcast(I32), 0)
@@ -97,12 +102,9 @@ def tile_picked_ywarrnt_min_po_kernel(
                 x_scales[:, 4 * q : 4 * q + 4, :].bitcast(I32),
             )
         w2_raw = load_words("w2_raw", w2_words)
-        x_table = []
-        for g in range(PASSES):
-            table = keep.tile([P, T], I32, name=f"x_table{g}", align_bytes=64)
-            nc.sync.dma_start(table[:], x_words[g].rearrange("p c r -> p (c r)").bitcast(I32))
-            x_table.append(table)
+        x_table = [load_table(0)]
         load_scales(w2_scale_rows, w2_scales)
+        x_table.append(load_table(1))
 
         xq_scales_0 = keep.tile([P, S], U8, name="xq_scales_0", align_bytes=64)
         nc.vector.tensor_copy(xq_scales_0[:], x_scale_rows[:].indirect(offs_sb[:]))

from contextlib import ExitStack

import concourse.mybir as mybir

K, T, S, N, H, U = 1024, 1024, 512, 512, 512, 1024
FLOPS = 2 * (2 * K * N * S + H * N * U)

F32 = mybir.dt.float32
BF16 = mybir.dt.bfloat16
I32 = mybir.dt.int32
U32 = mybir.dt.uint32
U16 = mybir.dt.uint16
U8 = mybir.dt.uint8
FP8X4 = mybir.dt.float8_e4m3fn_x4
FP4X4 = mybir.dt.float4_e2m1fn_x4
ALU = mybir.AluOpType
ACT = mybir.ActivationFunctionType

P = 128
PACK = 4
QUADS = 4
PASSES = K // (P * PACK)
BANK = 512
CHUNKS = (384, 256, 256, 128)
BLOCK = BANK // PACK
ON_VECTOR = (2, 0, 0, 0)
RUN = 4


def tile_picked_ywarrnt_min_po_kernel(
    tc, x_words, x_scales, w1_words, w1_scales, w2_words, w2_scales, unit, w3_words, w3_scales,
    offs, cl1, exc, def_, out_0, out_1, out_2,
):
    nc = tc.nc
    with ExitStack() as ctx:
        keep = ctx.enter_context(tc.tile_pool(name="keep", bufs=1))
        ring = ctx.enter_context(tc.tile_pool(name="ring", bufs=3))
        psum = ctx.enter_context(tc.psum_pool(name="psum", bufs=8))

        def load_list(name, src):
            lst = keep.tile(list(src.shape), U16, name=name)
            nc.sync.dma_start(lst[:], src)
            return lst

        def load_words(name, src):
            passes = src.shape[0]
            raw = keep.tile([P, passes * 2 * N], U8, name=name, align_bytes=64)
            nc.sync.dma_start(
                raw[:].bitcast(I32).rearrange("p (g c) -> p g c", g=passes),
                src.rearrange("g p c -> p g c").bitcast(I32),
            )
            return raw

        def load_table(g):
            table = keep.tile([P, T], I32, name=f"x_table{g}", align_bytes=64)
            nc.sync.dma_start(table[:], x_words[g].rearrange("p c r -> p (c r)").bitcast(I32))
            return table

        def zeroed(name, width, engine, tag=""):
            plane = keep.tile([P, width], U8, name=name, tag=tag, align_bytes=64)
            engine.memset(plane[:].bitcast(I32), 0)
            return plane

        def load_scales(raw, src):
            passes = src.shape[0]
            for q in range(QUADS):
                nc.sync.dma_start(
                    raw[32 * q : 32 * q + 4, :].bitcast(I32).rearrange("p (g c) -> p g c", g=passes),
                    src[:, 4 * q : 4 * q + 4, :].rearrange("g r c -> r g c").bitcast(I32),
                )

        def deal_words(name, raw, engine):
            dealt = keep.tile(list(raw.shape), U8, name=name, align_bytes=64)
            engine.tensor_copy(
                dealt[:].bitcast(U16).rearrange("p (t m) -> p t m", t=PACK),
                raw[:].bitcast(U16).rearrange("p (m t) -> p t m", t=PACK),
            )
            return dealt

        def deal_scales(name, raw, engine):
            dealt = keep.tile(list(raw.shape), U8, name=name, align_bytes=64)
            engine.tensor_copy(
                dealt[:].rearrange("p (t m) -> p t m", t=PACK),
                raw[:].rearrange("p (m t) -> p t m", t=PACK),
            )
            return dealt

        def stationary(words, scales, passes, t, g):
            at = (t * passes + g) * P
            return words[:, 2 * at : 2 * (at + P)].bitcast(FP4X4), scales[:, at : at + P]

        x_scale_rows = zeroed("x_scale_rows", T, nc.gpsimd)
        w2_scale_rows = zeroed("w2_scale_rows", PASSES * N, nc.vector, tag="shared")
        xq_scales_1 = zeroed("xq_scales_1", S, nc.gpsimd)
        w1_scale_rows = zeroed("w1_scale_rows", PASSES * N, nc.vector)
        w3_scale_rows = zeroed("w3_scale_rows", N, nc.gpsimd)

        offs_sb = load_list("offs_sb", offs)
        for q in range(QUADS):
            nc.sync.dma_start(
                x_scale_rows[32 * q : 32 * q + 4 * PASSES, :].bitcast(I32),
                x_scales[:, 4 * q : 4 * q + 4, :].bitcast(I32),
            )
        w2_raw = load_words("w2_raw", w2_words)
        x_table = [load_table(0)]
        load_scales(w2_scale_rows, w2_scales)
        x_table.append(load_table(1))

        xq_scales_0 = keep.tile([P, S], U8, name="xq_scales_0", align_bytes=64)
        nc.vector.tensor_copy(xq_scales_0[:], x_scale_rows[:].indirect(offs_sb[:]))
        for q in range(QUADS):
            nc.sync.dma_start(
                xq_scales_1[32 * q : 32 * q + 4, :].bitcast(I32),
                xq_scales_0[32 * q + 4 : 32 * q + 8, :].bitcast(I32),
            )
        xq_scales = (xq_scales_0, xq_scales_1)

        unit_sb = keep.tile([P, PACK], F32, name="unit_sb")
        nc.sync.dma_start(unit_sb[:], unit.rearrange("(p t) o -> p (t o)", t=PACK))
        w1_raw = load_words("w1_raw", w1_words)
        load_scales(w1_scale_rows, w1_scales)
        def_sb = load_list("def_sb", def_)
        cl1_sb = load_list("cl1_sb", cl1)
        exc_sb = load_list("exc_sb", exc)
        w3_raw = load_words("w3_raw", w3_words)
        load_scales(w3_scale_rows, w3_scales)

        unit_abs = keep.tile([P, PACK], F32, name="unit_abs")
        nc.scalar.activation(unit_abs[:], unit_sb[:], ACT.Abs)
        unit_sign = keep.tile([P, BLOCK * PACK], BF16, name="unit_sign")
        nc.scalar.activation(
            unit_sign[:].rearrange("p (r t) -> p r t", t=PACK),
            unit_sb[:].unsqueeze(1).to_broadcast([P, BLOCK, PACK]),
            ACT.Sign,
        )

        def picked_words(g, tag=""):
            picked = keep.tile([P, S], U32, name=f"xq_words{g}", tag=tag, align_bytes=64)
            nc.vector.tensor_copy(picked[:], x_table[g][:].bitcast(U32).indirect(offs_sb[:]))
            return picked

        def first_product(words, scales, t):
            bank = psum.tile([P, BANK], F32, name="bank")
            for g in range(PASSES):
                lhsT, lhsT_scale = stationary(words, scales, PASSES, t, g)
                nc.tensor.matmul_mx(
                    bank[:], lhsT=lhsT, lhsT_scale=lhsT_scale,
                    rhs=xq_words[g][:].bitcast(FP8X4), rhs_scale=xq_scales[g][:],
                    start=(g == 0), stop=(g == PASSES - 1),
                )
            return bank

        w2_dealt = deal_words("w2_dealt", w2_raw, nc.vector)
        xq_words = [picked_words(0)]
        w2_scale_dealt = deal_scales("w2_scale_dealt", w2_scale_rows, nc.vector)
        xq_words.append(picked_words(1, tag="shared"))
        w1_dealt = deal_words("w1_dealt", w1_raw, nc.vector)
        w1_scale_dealt = deal_scales("w1_scale_dealt", w1_scale_rows, nc.vector)
        w3_dealt = deal_words("w3_dealt", w3_raw, nc.vector)
        w3_scale_dealt = deal_scales("w3_scale_dealt", w3_scale_rows, nc.vector)

        z = [keep.tile([P, S], F32, name=f"z{t}") for t in range(PACK)]
        y = [keep.tile([P, S], F32, name=f"y{t}") for t in range(PACK)]
        z_banks, y_banks = [], []
        for t in range(PACK):
            z_banks.append(first_product(w2_dealt, w2_scale_dealt, t))
            y_banks.append(first_product(w1_dealt, w1_scale_dealt, t))

        out_codes = keep.tile([P, U], U32, name="out_codes", align_bytes=64)
        out_scales = keep.tile([P, U], U8, name="out_scales", align_bytes=64)
        out_rows = out_0.rearrange("(p t) r -> p t r", t=PACK)
        out_words = out_1[0].rearrange("p c r -> p (c r)").bitcast(I32)

        starts = [sum(CHUNKS[:c]) for c in range(len(CHUNKS))]
        st = [dict() for c in CHUNKS]

        def entries(lst, c):
            return lst[:, starts[c] // 16 : (starts[c] + CHUNKS[c]) // 16]

        def planes(ap):
            return ap.rearrange("p t (c i) -> p c t i", i=RUN)

        def woven(ap):
            return ap.rearrange("p (c i t) -> p c t i", i=RUN, t=PACK)

        def gather_def(c):
            st[c]["zd"] = []
            for t in range(PACK):
                if c == 0:
                    nc.scalar.activation(z[t][:], z_banks[t][:], ACT.Copy, scale=unit_abs[:, t : t + 1])
                zd = ring.tile([P, CHUNKS[c]], F32, name=f"zd{t}", bufs=2)
                nc.scalar.activation(zd[:], z[t][:].indirect(entries(def_sb, c)), ACT.Copy)
                st[c]["zd"].append(zd)
            st[c]["prod"] = ring.tile([P, PACK, CHUNKS[c]], F32, name="prod")

        def gather_exc(c):
            ze = ring.tile([P, PACK, CHUNKS[c]], F32, name="ze", bufs=2)
            for t in range(PACK):
                if t < ON_VECTOR[c]:
                    nc.vector.tensor_copy(ze[:, t, :], z[t][:].indirect(entries(exc_sb, c)))
                else:
                    nc.scalar.activation(ze[:, t, :], z[t][:].indirect(entries(exc_sb, c)), ACT.Copy)
            st[c]["ze"] = ze

        def gather_mult(c, t):
            if c == 0:
                nc.vector.tensor_copy(y[t][:], y_banks[t][:])
            nc.vector.tensor_tensor(
                st[c]["prod"][:, t, :], y[t][:].indirect(entries(cl1_sb, c)), st[c]["zd"][t][:], ALU.mult
            )

        def cut(c):
            mag = ring.tile([P, PACK * CHUNKS[c]], BF16, name="mag", align_bytes=64)
            nc.vector.tensor_tensor(woven(mag[:]), planes(st[c]["prod"][:]), planes(st[c]["ze"][:]), ALU.min)
            st[c]["mag"] = mag

        def signed(c):
            n = CHUNKS[c]
            hid = ring.tile([P, PACK * n], BF16, name="hid", align_bytes=64)
            nc.vector.tensor_tensor(
                hid[:].rearrange("p (b e) -> p b e", e=BLOCK * PACK),
                st[c]["mag"][:].rearrange("p (b e) -> p b e", e=BLOCK * PACK),
                unit_sign[:].unsqueeze(1).to_broadcast([P, n // BLOCK, BLOCK * PACK]),
                ALU.mult,
            )
            st[c]["hid"] = hid

        def last_product(c):
            n = CHUNKS[c]
            codes = ring.tile([P, n], U32, name="hid_codes", align_bytes=64)
            scales = ring.tile([P, n], U8, name="hid_scales", align_bytes=64)
            nc.vector.quantize_mx(codes[:].bitcast(FP8X4), scales[:], st[c]["hid"][:])
            banks = []
            for b0 in range(0, n, BLOCK):
                bank = psum.tile([P, PACK, BLOCK], F32, name="bank")
                for t in range(PACK):
                    lhsT, lhsT_scale = stationary(w3_dealt, w3_scale_dealt, 1, t, 0)
                    nc.tensor.matmul_mx(
                        bank[:, t, :], lhsT=lhsT, lhsT_scale=lhsT_scale,
                        rhs=codes[:, b0 : b0 + BLOCK].bitcast(FP8X4), rhs_scale=scales[:, b0 : b0 + BLOCK],
                        start=True, stop=True,
                    )
                banks.append(bank)
            st[c]["banks"] = banks

        def leave_psum(c):
            n = CHUNKS[c]
            res = ring.tile([P, PACK, n], F32, name="res", bufs=len(CHUNKS))
            for b, bank in enumerate(st[c]["banks"]):
                nc.scalar.copy(res[:, :, b * BLOCK : (b + 1) * BLOCK], bank[:])
            nc.sync.dma_start(out_rows[:, :, starts[c] : starts[c] + n], res[:])
            st[c]["res"] = res[:]

        def rounded(c):
            rnd = ring.tile([P, PACK * CHUNKS[c]], BF16, name="rnd", align_bytes=64)
            nc.vector.tensor_copy(woven(rnd[:]), planes(st[c]["res"]))
            st[c]["rnd"] = rnd

        def hand_on(c):
            cols = slice(starts[c], starts[c] + CHUNKS[c])
            nc.vector.quantize_mx(out_codes[:, cols].bitcast(FP8X4), out_scales[:, cols], st[c]["rnd"][:])
            nc.sync.dma_start(out_words[:, cols], out_codes[:, cols].bitcast(I32))

        last = len(CHUNKS) - 1
        for c in range(last + 4):
            here, one_back, three_back = c <= last, 1 <= c <= last + 1, c >= 3
            if here:
                gather_def(c)
                gather_mult(c, 0)
            if one_back:
                cut(c - 1)
            if here:
                gather_mult(c, 1)
            if one_back:
                signed(c - 1)
            if here:
                gather_mult(c, 2)
            if one_back:
                last_product(c - 1)
                leave_psum(c - 1)
            if here:
                gather_mult(c, 3)
            if three_back:
                rounded(c - 3)
            if here:
                gather_exc(c)
            if three_back:
                hand_on(c - 3)

        for q in range(QUADS):
            queue = nc.sync if q % 2 == 0 else nc.scalar
            queue.dma_start(
                out_2[0, 4 * q : 4 * q + 4, :].bitcast(I32),
                out_scales[32 * q : 32 * q + 4, :].bitcast(I32),
            )
